import numpy as np
import ml_dtypes


def mxq(x, axis, fmt="e4m3"):
    dtype, down = {"e4m3": (ml_dtypes.float8_e4m3fn, 7), "e5m2": (ml_dtypes.float8_e5m2, 14)}[fmt]
    v = np.moveaxis(np.asarray(x, np.float32).astype(ml_dtypes.bfloat16).astype(np.float64), axis, -1)
    blocks = v.reshape(v.shape[:-1] + (-1, 32))
    amax = np.abs(blocks).max(-1, keepdims=True)
    byte = np.maximum(np.where(amax > 0, np.frexp(amax)[1] - 1 + 127, 0) - down, 1)
    scale = np.exp2(byte - 127.0)
    codes = (blocks / scale).astype(np.float32).astype(dtype).astype(np.float64)
    return np.moveaxis((codes * scale).reshape(v.shape), -1, axis)


WIDE = False


def mx_kscale(k):
    if not WIDE:
        return np.ones(k)
    levels = np.array([10, -10, 5, -5, 0])
    if k % 512:
        return np.exp2(np.random.permutation(np.resize(levels, k // 32))).repeat(32)
    a = np.empty((k // 512, 16))
    for p in range(k // 512):
        a[p, :8] = np.random.permutation(np.resize(levels, 8))
        for g in range(8):
            far = levels[np.abs(levels - a[p, g]) >= 10]
            a[p, g + 8] = far[np.random.randint(len(far))]
    return np.exp2(a.ravel()).repeat(32)


def f64(x):
    return np.asarray(x).astype(np.float64)


def striped(idx):
    return np.tile(idx.reshape(-1, 16).T, (8, 1)).astype(np.uint16)


def unstriped(offs):
    return offs[:16].T.reshape(-1).astype(np.int64)


E2M1 = np.array([0.0, 0.5, 1.0, 1.5, 2.0, 3.0, 4.0, 6.0, -0.0, -0.5, -1.0, -1.5, -2.0, -3.0, -4.0, -6.0])


def pack_weight(w, fmt):
    k, n = w.shape
    w = f64(np.asarray(w, np.float32).astype(ml_dtypes.bfloat16)).reshape(k // 32, 32, n)
    amax = np.abs(w).max(1)
    if fmt == "e4m3":
        byte = np.frexp(amax)[1] - 1 + 127 - 7
    else:
        mant, ex = np.frexp(amax / 6.0)
        byte = np.where(mant > 0.5, ex, ex - 1) + 127
    byte = np.clip(np.where(amax > 0, byte, 1), 1, 254)
    scaled = (w * np.exp2(127.0 - byte)[:, None, :]).reshape(k, n).astype(np.float32)
    by_word = np.ascontiguousarray(scaled.reshape(k // 512, 128, 4, n).transpose(0, 1, 3, 2))
    if fmt == "e4m3":
        words = by_word.astype(ml_dtypes.float8_e4m3fn).view(np.uint8)
    else:
        c = by_word.astype(ml_dtypes.float4_e2m1fn).view(np.uint8) & 0xF
        words = (c[..., 0::2] | (c[..., 1::2] << 4)).reshape(k // 512, 128, 2 * n)
    return np.ascontiguousarray(words), np.ascontiguousarray(byte.astype(np.uint8).reshape(k // 512, 16, n))


def unpack_weight(words, scales, fmt):
    g, _, n = scales.shape
    words = np.ascontiguousarray(words).reshape(g, 128, n, -1)
    if fmt == "e4m3":
        vals = words.view(ml_dtypes.float8_e4m3fn).astype(np.float64)
    else:
        nib = np.empty((g, 128, n, 4), np.uint8)
        nib[..., 0::2] = words & 0xF
        nib[..., 1::2] = words >> 4
        vals = E2M1[nib]
    vals = vals * np.repeat(np.exp2(scales.astype(np.float64) - 127.0), 8, axis=1)[..., None]
    return vals.transpose(0, 1, 3, 2).reshape(g * 512, n)


def silu(v):
    return v / (1.0 + np.exp(-np.maximum(v, -700.0)))


K, T, E, C, N = 2560, 1024, 4, 128, 128
K8 = 1024


def by_expert(wq, xq):
    return np.concatenate([wq[e].T @ xq[:, e * C:(e + 1) * C] for e in range(E)], axis=1)


def setup_inputs():
    n = np.random.standard_normal
    s = mx_kscale(K)[:, None]
    w = n((E, K, N)) / np.sqrt(K) / s[None]
    w8 = [pack_weight(m[:K8], "e4m3") for m in w]
    w4 = [pack_weight(m[K8:], "e2m1") for m in w]
    return {
        "xT": (n((K, T)) * s).astype(np.float32),
        "xr": n((N, T)).astype(np.float32),
        "w8_words": np.stack([m[0] for m in w8]),
        "w8_scales": np.stack([m[1] for m in w8]),
        "w4_words": np.stack([m[0] for m in w4]),
        "w4_scales": np.stack([m[1] for m in w4]),
        "b": (0.3 * n((N, E))).astype(np.float32),
        "gate": np.tile(np.random.uniform(0.2, 1.0, E * C), (N, 1)).astype(np.float32),
        "offs": striped(np.random.permutation(T)[:E * C]),
    }


def reference(xT, xr, w8_words, w8_scales, w4_words, w4_scales, b, gate, offs):
    idx = unstriped(offs)
    w = np.stack([np.concatenate([unpack_weight(w8_words[e], w8_scales[e], "e4m3"), unpack_weight(w4_words[e], w4_scales[e], "e2m1")]) for e in range(E)])
    xq = mxq(f64(xT)[:, idx], 0, "e4m3")
    y = by_expert(w, xq)
    y = silu(y + np.repeat(f64(b), C, axis=1))
    out = f64(xr).copy()
    out[:, idx] += f64(gate) * y
    return out

@@ -1,0 +1,180 @@
+from contextlib import ExitStack
+
+import concourse.mybir as mybir
+
+F32 = mybir.dt.float32
+BF16 = mybir.dt.bfloat16
+U32 = mybir.dt.uint32
+I32 = mybir.dt.int32
+U16 = mybir.dt.uint16
+U8 = mybir.dt.uint8
+FP8X4 = mybir.dt.float8_e4m3fn_x4
+FP4X4 = mybir.dt.float4_e2m1fn_x4
+ACT = mybir.ActivationFunctionType
+ALU = mybir.AluOpType
+
+P = 128
+K, T, E, C, N = 2560, 1024, 4, 128, 128
+PASSES8, PASSES4 = 2, 3
+PASSES = PASSES8 + PASSES4
+SLOTS = E * C
+
+ORDER = ((0, 0, 4), (2, 0, 0), (3, 1, 0), (1, 2, 4), (4, 2, 0))
+SCALE_TILES = 3
+FIRST = ((0, 256), (256, 512), (512, 1024))
+MIDDLE = ((0, 512), (512, 1024))
+LAST = ((0, 512), (512, 768), (768, 1024))
+
+FLOPS = 2 * K * SLOTS * N
+
+
+def tile_moe_res_lin_silu_kernel(
+    tc, xT, xr, w8_words, w8_scales, w4_words, w4_scales, b, gate, offs, out
+):
+    nc = tc.nc
+    with ExitStack() as ctx:
+        keep = ctx.enter_context(tc.tile_pool(name="keep", bufs=1))
+        psum = ctx.enter_context(tc.psum_pool(name="psum", bufs=1))
+
+        offsets = keep.tile([P, SLOTS // 16], U16, name="offsets")
+        raw = [keep.tile([P, 4, T], F32, name=f"raw{g}") for g in range(PASSES)]
+        grouped = [keep.tile([P, T, 4], BF16, name=f"grouped{g}", align_bytes=64) for g in range(PASSES)]
+        words = [keep.tile([P, T], U32, name=f"words{g}", align_bytes=64) for g in range(PASSES)]
+        scales = [keep.tile([P, T], U8, name=f"scales{g}", align_bytes=64) for g in range(SCALE_TILES)]
+        slot_words = [keep.tile([P, SLOTS], U32, name=f"slot_words{g}", align_bytes=64) for g in range(PASSES)]
+        slot_scales = [keep.tile([P, SLOTS], U8, name=f"slot_scales{g}", align_bytes=64) for g in range(SCALE_TILES)]
+        w8 = keep.tile([P, E * PASSES8, 4 * N], U8, name="w8", align_bytes=64)
+        w4 = keep.tile([P, E * PASSES4, 2 * N], U8, name="w4", align_bytes=64)
+        w8s = keep.tile([P, E * PASSES8, N], U8, name="w8s", align_bytes=64)
+        w4s = keep.tile([P, E * PASSES4, N], U8, name="w4s", align_bytes=64)
+        bias = keep.tile([P, E], F32, name="bias")
+        gates = keep.tile([P, SLOTS], F32, name="gates")
+        residual = keep.tile([P, T], F32, name="residual")
+        y = keep.tile([P, SLOTS], F32, name="y")
+        scattered = keep.tile([P, T], F32, name="scattered")
+        result = keep.tile([P, T], F32, name="result")
+        warm = keep.tile([P, 8], F32, name="warm")
+        warm_out = keep.tile([P, 8], F32, name="warm_out")
+        acc = [psum.tile([P, C], F32, name=f"acc{e}") for e in range(E)]
+
+        nc.vector.memset(warm[:], 0.0)
+        nc.scalar.activation(warm_out[:], warm[:], ACT.Silu)
+        for g in range(SCALE_TILES):
+            nc.vector.memset(scales[g][:].bitcast(I32), 0)
+        nc.gpsimd.memset(w8s[:].bitcast(I32), 0)
+        nc.gpsimd.memset(w4s[:].bitcast(I32), 0)
+        nc.gpsimd.memset(scattered[:], 0.0)
+
+        chunks = []
+        for i in range(PASSES):
+            chunks += [(i, lo, hi) for lo, hi in (FIRST if i == 0 else LAST if i == PASSES - 1 else MIDDLE)]
+        for n, (i, lo, hi) in enumerate(chunks):
+            g = ORDER[i][0]
+            rows = xT[512 * g : 512 * (g + 1), lo:hi].rearrange("(p j) t -> p j t", j=4)
+            nc.sync.dma_start(raw[i][:, :, lo:hi], rows)
+            if n == 1:
+                nc.sync.dma_start(offsets[:], offs)
+                nc.sync.dma_start(bias[:], b)
+
+        for q in range(4):
+            nc.sync.dma_start(
+                w8s[32 * q : 32 * q + 4, :, :].bitcast(I32),
+                w8_scales[:, :, 4 * q : 4 * q + 4, :].rearrange("e a q n -> q (e a) n").bitcast(I32),
+            )
+            nc.sync.dma_start(
+                w4s[32 * q : 32 * q + 4, :, :].bitcast(I32),
+                w4_scales[:, :, 4 * q : 4 * q + 4, :].rearrange("e a q n -> q (e a) n").bitcast(I32),
+            )
+        nc.sync.dma_start(w8[:], w8_words.rearrange("e a p n r -> p (e a) (n r)"))
+        nc.sync.dma_start(w4[:], w4_words.rearrange("e a p n -> p (e a) n"))
+        nc.sync.dma_start(gates[:], gate)
+        nc.sync.dma_start(residual[:], xr)
+
+        def interleave(i, lo, hi, engine):
+            dst = grouped[i][:, lo:hi, :].rearrange("p (c i) t -> p c t i", i=4)
+            src = raw[i][:, :, lo:hi].rearrange("p t (c i) -> p c t i", i=4)
+            if engine == "scalar":
+                nc.scalar.activation(dst, src, ACT.Copy)
+            else:
+                nc.vector.tensor_copy(dst, src)
+
+        def quantise(i, lo, hi):
+            tile, row = ORDER[i][1:]
+            nc.vector.quantize_mx(
+                out=words[i][:, lo:hi].bitcast(FP8X4),
+                scales=scales[tile][row:P, lo:hi],
+                in_=grouped[i][:, lo:hi, :].rearrange("p t j -> p (t j)"),
+            )
+
+        def gather_words(i, lo, hi):
+            nc.vector.tensor_copy(slot_words[i][:, lo:hi], words[i][:].indirect(offsets[:, lo // 16 : hi // 16]))
+
+        def gather_scales(tile, lo, hi):
+            nc.vector.tensor_copy(slot_scales[tile][:, lo:hi], scales[tile][:].indirect(offsets[:, lo // 16 : hi // 16]))
+
+        def multiply(i, e):
+            g, tile, row = ORDER[i]
+            cols = slice(e * C, (e + 1) * C)
+            if g < PASSES8:
+                lhs = w8[:, e * PASSES8 + g, :].bitcast(FP8X4)
+                lhs_scale = w8s[:, e * PASSES8 + g, :]
+            else:
+                lhs = w4[:, e * PASSES4 + g - PASSES8, :].bitcast(FP4X4)
+                lhs_scale = w4s[:, e * PASSES4 + g - PASSES8, :]
+            nc.tensor.matmul_mx(
+                out=acc[e][:],
+                lhsT=lhs,
+                lhsT_scale=lhs_scale,
+                rhs=slot_words[i][:, cols].bitcast(FP8X4),
+                rhs_scale=slot_scales[tile][row:P, cols],
+                start=(i == 0),
+                stop=(i == PASSES - 1),
+            )
+
+        def scatter(lo, hi):
+            nc.vector.tensor_tensor(
+                scattered[:].indirect(offsets[:, lo // 16 : hi // 16]), y[:, lo:hi], gates[:, lo:hi], ALU.mult
+            )
+
+        members = [[i for i in range(PASSES) if ORDER[i][1] == tile] for tile in range(SCALE_TILES)]
+        pending = []
+        for n, (i, lo, hi) in enumerate(chunks):
+            last = i == PASSES - 1
+            mid = lo + (hi - lo) * (320 if last else 64) // 512
+            if mid < hi:
+                interleave(i, mid, hi, "scalar")
+            if mid > lo:
+                interleave(i, lo, mid, "vector")
+            for work in pending[:1]:
+                work()
+            pending = pending[1:]
+            quantise(i, lo, hi)
+            if hi == T and not last:
+                gather_words(i, 0, SLOTS)
+                tile = ORDER[i][1]
+                if members[tile][-1] == i:
+                    pending.append(lambda tile=tile: gather_scales(tile, 0, SLOTS))
+        for i in range(PASSES):
+            tile = ORDER[i][1]
+            if members[tile][-1] == i and i < PASSES - 1:
+                for m in members[tile]:
+                    for e in range(E):
+                        multiply(m, e)
+        i = PASSES - 1
+        tile = ORDER[i][1]
+        half = SLOTS // 2
+        for s in range(2):
+            gather_words(i, s * half, (s + 1) * half)
+            gather_scales(tile, s * half, (s + 1) * half)
+            for m in members[tile]:
+                for e in (2 * s, 2 * s + 1):
+                    multiply(m, e)
+            for e in (2 * s, 2 * s + 1):
+                cols = slice(e * C, (e + 1) * C)
+                nc.scalar.activation(y[:, cols], acc[e][:], ACT.Silu, bias=bias[:, e : e + 1])
+        scatter(0, half)
+        scatter(half, SLOTS)
+        for s in range(2):
+            cols = slice(s * T // 2, (s + 1) * T // 2)
+            nc.vector.tensor_tensor(result[:, cols], scattered[:, cols], residual[:, cols], ALU.add)
+            (nc.sync if s == 0 else nc.scalar).dma_start(out[:, cols], result[:, cols])

@@ -25,6 +25,8 @@ FIRST = ((0, 256), (256, 512), (512, 1024))
 MIDDLE = ((0, 512), (512, 1024))
 LAST = ((0, 512), (512, 768), (768, 1024))
 
+VECTOR_TOKENS = (64, 64, 128, 144, 144, 144, 144, 144, 176, 128, 128, 160)
+
 FLOPS = 2 * K * SLOTS * N
 
 
@@ -65,6 +67,16 @@ def tile_moe_res_lin_silu_kernel(
         nc.gpsimd.memset(w4s[:].bitcast(I32), 0)
         nc.gpsimd.memset(scattered[:], 0.0)
 
+        def load_scales(q):
+            nc.sync.dma_start(
+                w8s[32 * q : 32 * q + 4, :, :].bitcast(I32),
+                w8_scales[:, :, 4 * q : 4 * q + 4, :].rearrange("e a q n -> q (e a) n").bitcast(I32),
+            )
+            nc.sync.dma_start(
+                w4s[32 * q : 32 * q + 4, :, :].bitcast(I32),
+                w4_scales[:, :, 4 * q : 4 * q + 4, :].rearrange("e a q n -> q (e a) n").bitcast(I32),
+            )
+
         chunks = []
         for i in range(PASSES):
             chunks += [(i, lo, hi) for lo, hi in (FIRST if i == 0 else LAST if i == PASSES - 1 else MIDDLE)]
@@ -75,16 +87,9 @@ def tile_moe_res_lin_silu_kernel(
             if n == 1:
                 nc.sync.dma_start(offsets[:], offs)
                 nc.sync.dma_start(bias[:], b)
+            if 2 <= n < 2 + 4:
+                load_scales(n - 2)
 
-        for q in range(4):
-            nc.sync.dma_start(
-                w8s[32 * q : 32 * q + 4, :, :].bitcast(I32),
-                w8_scales[:, :, 4 * q : 4 * q + 4, :].rearrange("e a q n -> q (e a) n").bitcast(I32),
-            )
-            nc.sync.dma_start(
-                w4s[32 * q : 32 * q + 4, :, :].bitcast(I32),
-                w4_scales[:, :, 4 * q : 4 * q + 4, :].rearrange("e a q n -> q (e a) n").bitcast(I32),
-            )
         nc.sync.dma_start(w8[:], w8_words.rearrange("e a p n r -> p (e a) (n r)"))
         nc.sync.dma_start(w4[:], w4_words.rearrange("e a p n -> p (e a) n"))
         nc.sync.dma_start(gates[:], gate)
@@ -140,7 +145,7 @@ def tile_moe_res_lin_silu_kernel(
         pending = []
         for n, (i, lo, hi) in enumerate(chunks):
             last = i == PASSES - 1
-            mid = lo + (hi - lo) * (320 if last else 64) // 512
+            mid = lo + VECTOR_TOKENS[n]
             if mid < hi:
                 interleave(i, mid, hi, "scalar")
             if mid > lo:
@@ -174,7 +179,6 @@ def tile_moe_res_lin_silu_kernel(
                 nc.scalar.activation(y[:, cols], acc[e][:], ACT.Silu, bias=bias[:, e : e + 1])
         scatter(0, half)
         scatter(half, SLOTS)
-        for s in range(2):
-            cols = slice(s * T // 2, (s + 1) * T // 2)
-            nc.vector.tensor_tensor(result[:, cols], scattered[:, cols], residual[:, cols], ALU.add)
-            (nc.sync if s == 0 else nc.scalar).dma_start(out[:, cols], result[:, cols])
+        for n, (lo, hi) in enumerate(((0, 512), (512, 768), (768, 1024))):
+            nc.vector.tensor_tensor(result[:, lo:hi], scattered[:, lo:hi], residual[:, lo:hi], ALU.add)
+            (nc.sync if n % 2 == 0 else nc.scalar).dma_start(out[:, lo:hi], result[:, lo:hi])

@@ -21,11 +21,14 @@ SLOTS = E * C
 
 ORDER = ((0, 0, 4), (2, 0, 0), (3, 1, 0), (1, 2, 4), (4, 2, 0))
 SCALE_TILES = 3
-FIRST = ((0, 256), (256, 512), (512, 1024))
-MIDDLE = ((0, 512), (512, 1024))
-LAST = ((0, 512), (512, 768), (768, 1024))
-
-VECTOR_TOKENS = (64, 64, 128, 144, 144, 144, 144, 144, 176, 128, 128, 160)
+LOADS = (((0, 1024, 0, 2), (0, 1024, 2, 4)), ((0, 1024, 0, 4),), ((0, 1024, 0, 4),), ((0, 1024, 0, 4),), ((0, 512, 0, 4), (512, 768, 0, 4), (768, 1024, 0, 4)))
+UNITS = (
+    (((0, 128, 512), (512, 640, 1024)),),
+    (((0, 128, 512), (512, 640, 1024)),),
+    (((0, 128, 512), (512, 640, 1024)),),
+    (((0, 256, 512), (512, 768, 1024)),),
+    (((0, 160, 512),), ((512, 640, 768),), ((768, 928, 1024),)),
+)
 
 FLOPS = 2 * K * SLOTS * N
 
@@ -77,18 +80,18 @@ def tile_moe_res_lin_silu_kernel(
                 w4_scales[:, :, 4 * q : 4 * q + 4, :].rearrange("e a q n -> q (e a) n").bitcast(I32),
             )
 
-        chunks = []
+        n = 0
         for i in range(PASSES):
-            chunks += [(i, lo, hi) for lo, hi in (FIRST if i == 0 else LAST if i == PASSES - 1 else MIDDLE)]
-        for n, (i, lo, hi) in enumerate(chunks):
+          for lo, hi, j0, j1 in LOADS[i]:
             g = ORDER[i][0]
             rows = xT[512 * g : 512 * (g + 1), lo:hi].rearrange("(p j) t -> p j t", j=4)
-            nc.sync.dma_start(raw[i][:, :, lo:hi], rows)
-            if n == 1:
+            nc.sync.dma_start(raw[i][:, j0:j1, lo:hi], rows[:, j0:j1, :])
+            n += 1
+            if n == 2:
                 nc.sync.dma_start(offsets[:], offs)
                 nc.sync.dma_start(bias[:], b)
-            if 2 <= n < 2 + 4:
-                load_scales(n - 2)
+            if 3 <= n < 3 + 4:
+                load_scales(n - 3)
 
         nc.sync.dma_start(w8[:], w8_words.rearrange("e a p n r -> p (e a) (n r)"))
         nc.sync.dma_start(w4[:], w4_words.rearrange("e a p n -> p (e a) n"))
@@ -143,18 +146,19 @@ def tile_moe_res_lin_silu_kernel(
 
         members = [[i for i in range(PASSES) if ORDER[i][1] == tile] for tile in range(SCALE_TILES)]
         pending = []
-        for n, (i, lo, hi) in enumerate(chunks):
-            last = i == PASSES - 1
-            mid = lo + VECTOR_TOKENS[n]
-            if mid < hi:
-                interleave(i, mid, hi, "scalar")
-            if mid > lo:
-                interleave(i, lo, mid, "vector")
+        for i in range(PASSES):
+          for group in UNITS[i]:
+            for lo, mid, hi in group:
+                if mid < hi:
+                    interleave(i, mid, hi, "scalar")
+                if mid > lo:
+                    interleave(i, lo, mid, "vector")
             for work in pending[:1]:
                 work()
             pending = pending[1:]
-            quantise(i, lo, hi)
-            if hi == T and not last:
+            for lo, mid, hi in group:
+                quantise(i, lo, hi)
+            if group[-1][2] == T and i < PASSES - 1:
                 gather_words(i, 0, SLOTS)
                 tile = ORDER[i][1]
                 if members[tile][-1] == i:

@@ -19,15 +19,15 @@ PASSES8, PASSES4 = 2, 3
 PASSES = PASSES8 + PASSES4
 SLOTS = E * C
 
-ORDER = ((0, 0, 4), (2, 0, 0), (3, 1, 0), (1, 2, 4), (4, 2, 0))
+ORDER = ((2, 0, 0), (3, 1, 0), (0, 2, 4), (1, 2, 8), (4, 2, 0))
 SCALE_TILES = 3
-LOADS = (((0, 1024, 0, 2), (0, 1024, 2, 4)), ((0, 1024, 0, 4),), ((0, 1024, 0, 4),), ((0, 1024, 0, 4),), ((0, 512, 0, 4), (512, 768, 0, 4), (768, 1024, 0, 4)))
+LOADS = (((0, 1024),),) * 4 + (((0, 512), (512, 768), (768, 1024)),)
 UNITS = (
-    (((0, 128, 512), (512, 640, 1024)),),
-    (((0, 128, 512), (512, 640, 1024)),),
-    (((0, 128, 512), (512, 640, 1024)),),
-    (((0, 256, 512), (512, 768, 1024)),),
-    (((0, 160, 512),), ((512, 640, 768),), ((768, 928, 1024),)),
+    (((0, 320, 512), (512, 816, 1024)),),
+    (((0, 320, 512), (512, 704, 1024)),),
+    (((0, 224, 512), (512, 736, 1024)),),
+    (((0, 176, 512), (512, 880, 1024)),),
+    (((0, 192, 512),), ((512, 512, 768),), ((768, 896, 1024),)),
 )
 
 FLOPS = 2 * K * SLOTS * N
@@ -42,7 +42,10 @@ def tile_moe_res_lin_silu_kernel(
         psum = ctx.enter_context(tc.psum_pool(name="psum", bufs=1))
 
         offsets = keep.tile([P, SLOTS // 16], U16, name="offsets")
-        raw = [keep.tile([P, 4, T], F32, name=f"raw{g}") for g in range(PASSES)]
+        raw = [
+            [(lo, hi, keep.tile([P, 4, hi - lo], F32, name=f"raw{i}_{lo}")) for lo, hi in LOADS[i]]
+            for i in range(PASSES)
+        ]
         grouped = [keep.tile([P, T, 4], BF16, name=f"grouped{g}", align_bytes=64) for g in range(PASSES)]
         words = [keep.tile([P, T], U32, name=f"words{g}", align_bytes=64) for g in range(PASSES)]
         scales = [keep.tile([P, T], U8, name=f"scales{g}", align_bytes=64) for g in range(SCALE_TILES)]
@@ -70,37 +73,33 @@ def tile_moe_res_lin_silu_kernel(
         nc.gpsimd.memset(w4s[:].bitcast(I32), 0)
         nc.gpsimd.memset(scattered[:], 0.0)
 
-        def load_scales(q):
+        def load_scales(planes, codes_scales, q):
             nc.sync.dma_start(
-                w8s[32 * q : 32 * q + 4, :, :].bitcast(I32),
-                w8_scales[:, :, 4 * q : 4 * q + 4, :].rearrange("e a q n -> q (e a) n").bitcast(I32),
-            )
-            nc.sync.dma_start(
-                w4s[32 * q : 32 * q + 4, :, :].bitcast(I32),
-                w4_scales[:, :, 4 * q : 4 * q + 4, :].rearrange("e a q n -> q (e a) n").bitcast(I32),
+                planes[32 * q : 32 * q + 4, :, :].bitcast(I32),
+                codes_scales[:, :, 4 * q : 4 * q + 4, :].rearrange("e a q n -> q (e a) n").bitcast(I32),
             )
 
-        n = 0
         for i in range(PASSES):
-          for lo, hi, j0, j1 in LOADS[i]:
             g = ORDER[i][0]
-            rows = xT[512 * g : 512 * (g + 1), lo:hi].rearrange("(p j) t -> p j t", j=4)
-            nc.sync.dma_start(raw[i][:, j0:j1, lo:hi], rows[:, j0:j1, :])
-            n += 1
-            if n == 2:
+            for lo, hi, tile in raw[i]:
+                rows = xT[512 * g : 512 * (g + 1), lo:hi].rearrange("(p j) t -> p j t", j=4)
+                nc.sync.dma_start(tile[:], rows)
+            if i == 0:
                 nc.sync.dma_start(offsets[:], offs)
                 nc.sync.dma_start(bias[:], b)
-            if 3 <= n < 3 + 4:
-                load_scales(n - 3)
-
-        nc.sync.dma_start(w8[:], w8_words.rearrange("e a p n r -> p (e a) (n r)"))
+                for q in range(4):
+                    load_scales(w8s, w8_scales, q)
+        for q in range(4):
+            load_scales(w4s, w4_scales, q)
         nc.sync.dma_start(w4[:], w4_words.rearrange("e a p n -> p (e a) n"))
+        nc.sync.dma_start(w8[:], w8_words.rearrange("e a p n r -> p (e a) (n r)"))
         nc.sync.dma_start(gates[:], gate)
         nc.sync.dma_start(residual[:], xr)
 
         def interleave(i, lo, hi, engine):
             dst = grouped[i][:, lo:hi, :].rearrange("p (c i) t -> p c t i", i=4)
-            src = raw[i][:, :, lo:hi].rearrange("p t (c i) -> p c t i", i=4)
+            first, tile = [(f, t) for f, end, t in raw[i] if f <= lo and hi <= end][0]
+            src = tile[:, :, lo - first : hi - first].rearrange("p t (c i) -> p c t i", i=4)
             if engine == "scalar":
                 nc.scalar.activation(dst, src, ACT.Copy)
             else:
@@ -145,30 +144,24 @@ def tile_moe_res_lin_silu_kernel(
             )
 
         members = [[i for i in range(PASSES) if ORDER[i][1] == tile] for tile in range(SCALE_TILES)]
-        pending = []
         for i in range(PASSES):
-          for group in UNITS[i]:
-            for lo, mid, hi in group:
-                if mid < hi:
-                    interleave(i, mid, hi, "scalar")
-                if mid > lo:
-                    interleave(i, lo, mid, "vector")
-            for work in pending[:1]:
-                work()
-            pending = pending[1:]
-            for lo, mid, hi in group:
-                quantise(i, lo, hi)
-            if group[-1][2] == T and i < PASSES - 1:
+            for group in UNITS[i]:
+                for lo, mid, hi in group:
+                    if mid < hi:
+                        interleave(i, mid, hi, "scalar")
+                    if mid > lo:
+                        interleave(i, lo, mid, "vector")
+                if i == PASSES - 1 and group is UNITS[i][0]:
+                    gather_words(i - 1, 0, SLOTS)
+                for lo, mid, hi in group:
+                    quantise(i, lo, hi)
+            if i < PASSES - 2:
                 gather_words(i, 0, SLOTS)
                 tile = ORDER[i][1]
-                if members[tile][-1] == i:
-                    pending.append(lambda tile=tile: gather_scales(tile, 0, SLOTS))
-        for i in range(PASSES):
-            tile = ORDER[i][1]
-            if members[tile][-1] == i and i < PASSES - 1:
-                for m in members[tile]:
+                if members[tile] == [i]:
+                    gather_scales(tile, 0, SLOTS)
                     for e in range(E):
-                        multiply(m, e)
+                        multiply(i, e)
         i = PASSES - 1
         tile = ORDER[i][1]
         half = SLOTS // 2

from contextlib import ExitStack

import concourse.mybir as mybir

F32 = mybir.dt.float32
BF16 = mybir.dt.bfloat16
U32 = mybir.dt.uint32
I32 = mybir.dt.int32
U16 = mybir.dt.uint16
U8 = mybir.dt.uint8
FP8X4 = mybir.dt.float8_e4m3fn_x4
FP4X4 = mybir.dt.float4_e2m1fn_x4
ACT = mybir.ActivationFunctionType
ALU = mybir.AluOpType

P = 128
K, T, E, C, N = 2560, 1024, 4, 128, 128
PASSES8, PASSES4 = 2, 3
PASSES = PASSES8 + PASSES4
SLOTS = E * C

ORDER = ((2, 0, 0), (3, 1, 0), (0, 2, 4), (1, 2, 8), (4, 2, 0))
SCALE_TILES = 3
LOADS = (((0, 1024),),) * 4 + (((0, 512), (512, 768), (768, 1024)),)
UNITS = (
    (((0, 320, 512), (512, 816, 1024)),),
    (((0, 320, 512), (512, 704, 1024)),),
    (((0, 224, 512), (512, 736, 1024)),),
    (((0, 176, 512), (512, 880, 1024)),),
    (((0, 192, 512),), ((512, 512, 768),), ((768, 896, 1024),)),
)

FLOPS = 2 * K * SLOTS * N


def tile_moe_res_lin_silu_kernel(
    tc, xT, xr, w8_words, w8_scales, w4_words, w4_scales, b, gate, offs, out
):
    nc = tc.nc
    with ExitStack() as ctx:
        keep = ctx.enter_context(tc.tile_pool(name="keep", bufs=1))
        psum = ctx.enter_context(tc.psum_pool(name="psum", bufs=1))

        offsets = keep.tile([P, SLOTS // 16], U16, name="offsets")
        raw = [
            [(lo, hi, keep.tile([P, 4, hi - lo], F32, name=f"raw{i}_{lo}")) for lo, hi in LOADS[i]]
            for i in range(PASSES)
        ]
        grouped = [keep.tile([P, T, 4], BF16, name=f"grouped{g}", align_bytes=64) for g in range(PASSES)]
        words = [keep.tile([P, T], U32, name=f"words{g}", align_bytes=64) for g in range(PASSES)]
        scales = [keep.tile([P, T], U8, name=f"scales{g}", align_bytes=64) for g in range(SCALE_TILES)]
        slot_words = [keep.tile([P, SLOTS], U32, name=f"slot_words{g}", align_bytes=64) for g in range(PASSES)]
        slot_scales = [keep.tile([P, SLOTS], U8, name=f"slot_scales{g}", align_bytes=64) for g in range(SCALE_TILES)]
        w8 = keep.tile([P, E * PASSES8, 4 * N], U8, name="w8", align_bytes=64)
        w4 = keep.tile([P, E * PASSES4, 2 * N], U8, name="w4", align_bytes=64)
        w8s = keep.tile([P, E * PASSES8, N], U8, name="w8s", align_bytes=64)
        w4s = keep.tile([P, E * PASSES4, N], U8, name="w4s", align_bytes=64)
        bias = keep.tile([P, E], F32, name="bias")
        gates = keep.tile([P, SLOTS], F32, name="gates")
        residual = keep.tile([P, T], F32, name="residual")
        y = keep.tile([P, SLOTS], F32, name="y")
        scattered = keep.tile([P, T], F32, name="scattered")
        result = keep.tile([P, T], F32, name="result")
        warm = keep.tile([P, 8], F32, name="warm")
        warm_out = keep.tile([P, 8], F32, name="warm_out")
        acc = [psum.tile([P, C], F32, name=f"acc{e}") for e in range(E)]

        nc.vector.memset(warm[:], 0.0)
        nc.scalar.activation(warm_out[:], warm[:], ACT.Silu)
        for g in range(SCALE_TILES):
            nc.vector.memset(scales[g][:].bitcast(I32), 0)
        nc.gpsimd.memset(w8s[:].bitcast(I32), 0)
        nc.gpsimd.memset(w4s[:].bitcast(I32), 0)
        nc.gpsimd.memset(scattered[:], 0.0)

        def load_scales(planes, codes_scales, q):
            nc.sync.dma_start(
                planes[32 * q : 32 * q + 4, :, :].bitcast(I32),
                codes_scales[:, :, 4 * q : 4 * q + 4, :].rearrange("e a q n -> q (e a) n").bitcast(I32),
            )

        for i in range(PASSES):
            g = ORDER[i][0]
            for lo, hi, tile in raw[i]:
                rows = xT[512 * g : 512 * (g + 1), lo:hi].rearrange("(p j) t -> p j t", j=4)
                nc.sync.dma_start(tile[:], rows)
            if i == 0:
                nc.sync.dma_start(offsets[:], offs)
                nc.sync.dma_start(bias[:], b)
                for q in range(4):
                    load_scales(w8s, w8_scales, q)
        for q in range(4):
            load_scales(w4s, w4_scales, q)
        nc.sync.dma_start(w4[:], w4_words.rearrange("e a p n -> p (e a) n"))
        nc.sync.dma_start(w8[:], w8_words.rearrange("e a p n r -> p (e a) (n r)"))
        nc.sync.dma_start(gates[:], gate)
        nc.sync.dma_start(residual[:], xr)

        def interleave(i, lo, hi, engine):
            dst = grouped[i][:, lo:hi, :].rearrange("p (c i) t -> p c t i", i=4)
            first, tile = [(f, t) for f, end, t in raw[i] if f <= lo and hi <= end][0]
            src = tile[:, :, lo - first : hi - first].rearrange("p t (c i) -> p c t i", i=4)
            if engine == "scalar":
                nc.scalar.activation(dst, src, ACT.Copy)
            else:
                nc.vector.tensor_copy(dst, src)

        def quantise(i, lo, hi):
            tile, row = ORDER[i][1:]
            nc.vector.quantize_mx(
                out=words[i][:, lo:hi].bitcast(FP8X4),
                scales=scales[tile][row:P, lo:hi],
                in_=grouped[i][:, lo:hi, :].rearrange("p t j -> p (t j)"),
            )

        def gather_words(i, lo, hi):
            nc.vector.tensor_copy(slot_words[i][:, lo:hi], words[i][:].indirect(offsets[:, lo // 16 : hi // 16]))

        def gather_scales(tile, lo, hi):
            nc.vector.tensor_copy(slot_scales[tile][:, lo:hi], scales[tile][:].indirect(offsets[:, lo // 16 : hi // 16]))

        def multiply(i, e):
            g, tile, row = ORDER[i]
            cols = slice(e * C, (e + 1) * C)
            if g < PASSES8:
                lhs = w8[:, e * PASSES8 + g, :].bitcast(FP8X4)
                lhs_scale = w8s[:, e * PASSES8 + g, :]
            else:
                lhs = w4[:, e * PASSES4 + g - PASSES8, :].bitcast(FP4X4)
                lhs_scale = w4s[:, e * PASSES4 + g - PASSES8, :]
            nc.tensor.matmul_mx(
                out=acc[e][:],
                lhsT=lhs,
                lhsT_scale=lhs_scale,
                rhs=slot_words[i][:, cols].bitcast(FP8X4),
                rhs_scale=slot_scales[tile][row:P, cols],
                start=(i == 0),
                stop=(i == PASSES - 1),
            )

        def scatter(lo, hi):
            nc.vector.tensor_tensor(
                scattered[:].indirect(offsets[:, lo // 16 : hi // 16]), y[:, lo:hi], gates[:, lo:hi], ALU.mult
            )

        members = [[i for i in range(PASSES) if ORDER[i][1] == tile] for tile in range(SCALE_TILES)]
        for i in range(PASSES):
            for group in UNITS[i]:
                for lo, mid, hi in group:
                    if mid < hi:
                        interleave(i, mid, hi, "scalar")
                    if mid > lo:
                        interleave(i, lo, mid, "vector")
                if i == PASSES - 1 and group is UNITS[i][0]:
                    gather_words(i - 1, 0, SLOTS)
                for lo, mid, hi in group:
                    quantise(i, lo, hi)
            if i < PASSES - 2:
                gather_words(i, 0, SLOTS)
                tile = ORDER[i][1]
                if members[tile] == [i]:
                    gather_scales(tile, 0, SLOTS)
                    for e in range(E):
                        multiply(i, e)
        i = PASSES - 1
        tile = ORDER[i][1]
        half = SLOTS // 2
        for s in range(2):
            gather_words(i, s * half, (s + 1) * half)
            gather_scales(tile, s * half, (s + 1) * half)
            for m in members[tile]:
                for e in (2 * s, 2 * s + 1):
                    multiply(m, e)
            for e in (2 * s, 2 * s + 1):
                cols = slice(e * C, (e + 1) * C)
                nc.scalar.activation(y[:, cols], acc[e][:], ACT.Silu, bias=bias[:, e : e + 1])
        scatter(0, half)
        scatter(half, SLOTS)
        for n, (lo, hi) in enumerate(((0, 512), (512, 768), (768, 1024))):
            nc.vector.tensor_tensor(result[:, lo:hi], scattered[:, lo:hi], residual[:, lo:hi], ALU.add)
            (nc.sync if n % 2 == 0 else nc.scalar).dma_start(out[:, lo:hi], result[:, lo:hi])
